import numpy as np
import ml_dtypes


def mxq(x, axis, fmt="e4m3"):
    dtype, down = {"e4m3": (ml_dtypes.float8_e4m3fn, 7), "e5m2": (ml_dtypes.float8_e5m2, 14)}[fmt]
    v = np.moveaxis(np.asarray(x, np.float32).astype(ml_dtypes.bfloat16).astype(np.float64), axis, -1)
    blocks = v.reshape(v.shape[:-1] + (-1, 32))
    amax = np.abs(blocks).max(-1, keepdims=True)
    byte = np.maximum(np.where(amax > 0, np.frexp(amax)[1] - 1 + 127, 0) - down, 1)
    scale = np.exp2(byte - 127.0)
    codes = (blocks / scale).astype(np.float32).astype(dtype).astype(np.float64)
    return np.moveaxis((codes * scale).reshape(v.shape), -1, axis)


WIDE = False


def mx_kscale(k):
    if not WIDE:
        return np.ones(k)
    levels = np.array([10, -10, 5, -5, 0])
    if k % 512:
        return np.exp2(np.random.permutation(np.resize(levels, k // 32))).repeat(32)
    a = np.empty((k // 512, 16))
    for p in range(k // 512):
        a[p, :8] = np.random.permutation(np.resize(levels, 8))
        for g in range(8):
            far = levels[np.abs(levels - a[p, g]) >= 10]
            a[p, g + 8] = far[np.random.randint(len(far))]
    return np.exp2(a.ravel()).repeat(32)


BF16 = ml_dtypes.bfloat16


def bf(x):
    return np.asarray(x, np.float32).astype(BF16)


def f64(x):
    return np.asarray(x).astype(np.float64)


E2M1 = np.array([0.0, 0.5, 1.0, 1.5, 2.0, 3.0, 4.0, 6.0, -0.0, -0.5, -1.0, -1.5, -2.0, -3.0, -4.0, -6.0])


def pack_weight(w, fmt):
    k, n = w.shape
    w = f64(bf(w)).reshape(k // 32, 32, n)
    amax = np.abs(w).max(1)
    if fmt == "e4m3":
        byte = np.frexp(amax)[1] - 1 + 127 - 7
    else:
        mant, ex = np.frexp(amax / 6.0)
        byte = np.where(mant > 0.5, ex, ex - 1) + 127
    byte = np.clip(np.where(amax > 0, byte, 1), 1, 254)
    scaled = (w * np.exp2(127.0 - byte)[:, None, :]).reshape(k, n).astype(np.float32)
    by_word = np.ascontiguousarray(scaled.reshape(k // 512, 128, 4, n).transpose(0, 1, 3, 2))
    if fmt == "e4m3":
        words = by_word.astype(ml_dtypes.float8_e4m3fn).view(np.uint8)
    else:
        c = by_word.astype(ml_dtypes.float4_e2m1fn).view(np.uint8) & 0xF
        words = c[..., 0::2] | (c[..., 1::2] << 4)
    return np.ascontiguousarray(words), np.ascontiguousarray(byte.astype(np.uint8).reshape(k // 512, 16, n))


def unpack_weight(words, scales, fmt):
    g, p, n, _ = words.shape
    if fmt == "e4m3":
        vals = np.ascontiguousarray(words).view(ml_dtypes.float8_e4m3fn).astype(np.float64)
    else:
        nib = np.empty((g, p, n, 4), np.uint8)
        nib[..., 0::2] = words & 0xF
        nib[..., 1::2] = words >> 4
        vals = E2M1[nib]
    vals = vals * np.repeat(np.exp2(scales.astype(np.float64) - 127.0), 8, axis=1)[..., None]
    return vals.transpose(0, 1, 3, 2).reshape(g * 512, n)
def pack4(w):
    words, scales = pack_weight(w, "e2m1")
    return words.reshape(words.shape[0], 128, -1), scales


def unpack4(words, scales):
    return unpack_weight(words.reshape(words.shape[0], 128, -1, 2), scales, "e2m1")


def planes(Y):
    n, m = Y.shape
    b = f64(bf(Y)).reshape(n // 32, 32, m)
    amax = np.abs(b).max(1)
    byte = np.clip(np.where(amax > 0, np.frexp(amax)[1] - 1 + 127 - 7, 1), 1, 254)
    codes = (b * np.exp2(127.0 - byte)[:, None, :]).reshape(n, m).astype(np.float32).astype(ml_dtypes.float8_e4m3fn).view(np.uint8)
    words = codes.reshape(n // 512, 128, 4, m).transpose(0, 1, 3, 2)
    return np.ascontiguousarray(words), np.ascontiguousarray(byte.astype(np.uint8).reshape(n // 512, 16, m))


G, R, I, O = 4, 512, 512, 1024
SPAN = 1.5

def setup_inputs():
    u = np.random.uniform(-SPAN, SPAN, (G, I, 1))
    v = np.random.uniform(-SPAN, SPAN, (G, 1, O))
    w = np.random.uniform(-SPAN, SPAN, (G, R, 1))
    chan = np.exp(u * v + 0.5 * np.random.randn(G, I, O) + 0.6 * np.random.randn(G, 1, O))
    chan = chan / chan.mean(axis=2, keepdims=True)
    prior = np.exp(w * u.reshape(G, 1, I) + 0.5 * np.random.randn(G, R, I))
    prior = prior / prior.mean(axis=2, keepdims=True)
    gain = np.random.uniform(0.5, 2.5, (G, O))
    self_term = (gain.reshape(G, 1, O) * chan * np.log(chan)).mean(axis=2)
    factor = np.exp(0.8 * np.random.randn(G, I))
    s = mx_kscale(G * I).reshape(G, I)
    t = mx_kscale(G * O).reshape(G, O)
    fwd_words, fwd_scales = pack4((chan / I / s.reshape(G, I, 1)).reshape(G * I, O))
    bwd_words, bwd_scales = pack4((chan.swapaxes(1, 2) / O / t.reshape(G, O, 1)).reshape(G * O, I))
    return {"prior": bf(prior * s.reshape(G, 1, I)), "fwd_words": fwd_words, "fwd_scales": fwd_scales,
            "bwd_words": bwd_words, "bwd_scales": bwd_scales, "log_gain": bf(gain * t),
            "self_term": bf(self_term), "input_factor": bf(factor / s)}

def reference(prior, fwd_words, fwd_scales, bwd_words, bwd_scales, log_gain, self_term, input_factor):
    prior = f64(prior)
    fwd = unpack4(fwd_words, fwd_scales).reshape(G, I, O)
    bwd = unpack4(bwd_words, bwd_scales).reshape(G, O, I)
    mix = mxq(prior, 2, "e4m3") @ fwd
    wlog = np.log(mix) * f64(log_gain).reshape(G, 1, O)
    cross = mxq(wlog, 2, "e4m3") @ bwd
    y = prior * np.exp(f64(self_term).reshape(G, 1, I) - cross) * f64(input_factor).reshape(G, 1, I)
    Y = y.reshape(G * R, I).T
    words, scales = planes(Y)
    return y, words, scales

from contextlib import ExitStack

import concourse.mybir as mybir
from concourse.masks import make_identity

G, R, I, O = 4, 512, 512, 1024
FLOPS = 2 * G * R * I * O * 2

F32 = mybir.dt.float32
BF16 = mybir.dt.bfloat16
I32 = mybir.dt.int32
U32 = mybir.dt.uint32
U8 = mybir.dt.uint8
FP8X4 = mybir.dt.float8_e4m3fn_x4
FP4X4 = mybir.dt.float4_e2m1fn_x4
ACT = mybir.ActivationFunctionType
ALU = mybir.AluOpType

P = 128
UNITS = 2 * G
TILES = 2 * UNITS


def tile_log_output_prior_update_k7_kernel(
    tc, prior, fwd_words, fwd_scales, bwd_words, bwd_scales, log_gain, self_term, input_factor, out_0, out_1, out_2
):
    nc = tc.nc
    with ExitStack() as ctx:
        keep = ctx.enter_context(tc.tile_pool(name="keep", bufs=1))
        psum = ctx.enter_context(tc.psum_pool(name="psum", bufs=1))
        ctx.enter_context(nc.allow_non_contiguous_dma(reason="small per-partition vectors"))
        ctx.enter_context(tc.manual_schedule())

        def tiles(name, count, shape, dtype):
            return [keep.tile(shape, dtype, name="%s%d" % (name, n), align_bytes=64) for n in range(count)]

        prior_sb = tiles("prior", UNITS, [P, 2, I], BF16)
        f_words = tiles("f_words", G, [P, 2 * O], U8)
        b_words = tiles("b_words", G, [P, 2, 2 * I], U8)
        f_scales_first = keep.tile([P, 1, O], U8, align_bytes=64)
        f_scales_rest = keep.tile([P, G - 1, O], U8, align_bytes=64)
        b_scales = keep.tile([P, 2 * G, I], U8, align_bytes=64)
        gain_first = keep.tile([P, 2, 4], BF16)
        gain_rest = keep.tile([P, 2 * (G - 1), 4], BF16)
        self_raw = keep.tile([P, 4 * G, 2], BF16)
        factor_raw = keep.tile([P, 4 * G, 2], BF16)
        self_col = keep.tile([P, 4 * G], F32)
        factor_col = keep.tile([P, 4 * G], F32)
        ident = keep.tile([P, P], F32)
        warm = keep.tile([P, 1], F32)

        prior_t = tiles("prior_t", TILES, [P, 512], BF16)
        p_codes = tiles("p_codes", TILES, [P, P], U32)
        p_scales = tiles("p_scales", TILES, [P, P], U8)
        logs = tiles("logs", 16, [P, 512], F32)
        wlog = tiles("wlog", 2 * UNITS, [P, 1024], BF16)
        w_codes = tiles("w_codes", 2 * G, [P, 512], U32)
        w_scales = tiles("w_scales", 2 * G, [P, 512], U8)
        expo = logs
        y_sb = tiles("y_sb", UNITS, [P, 2, I], F32)
        y_bf = wlog[:UNITS]
        y_t = wlog[UNITS:]
        y_codes = tiles("y_codes", G, [P, 512], U32)
        y_scales = keep.tile([P, G * R], U8, align_bytes=64)

        banks = {}
        turn = {"mx": 0, "tr": 0}

        def new_bank(kind, key):
            n = turn[kind] % 4
            banks[key] = psum.tile([P, 512], F32, name="%s_bank" % kind, tag="%s%d" % (kind, n))
            turn[kind] = turn[kind] + 1
            return banks[key]

        def load_prior(u):
            c, h = divmod(u, 2)
            nc.sync.dma_start(
                out=prior_sb[u][:], in_=prior[c, 256 * h : 256 * (h + 1), :].rearrange("(p e) i -> p e i", e=2)
            )

        def load_f(c):
            nc.sync.dma_start(out=f_words[c][:].bitcast(I32), in_=fwd_words[c].bitcast(I32))

        def load_b(c):
            nc.sync.dma_start(
                out=b_words[c][:].bitcast(I32),
                in_=bwd_words[2 * c : 2 * c + 2].rearrange("g p n -> p g n").bitcast(I32),
            )

        def load_scales(plane, rows):
            for q in range(4):
                nc.sync.dma_start(
                    out=plane[32 * q : 32 * q + 4].bitcast(I32),
                    in_=rows[:, 4 * q : 4 * q + 4, :].rearrange("g r n -> r g n").bitcast(I32),
                )

        nc.vector.memset(f_scales_first[:].bitcast(I32), 0)
        nc.vector.memset(warm[:], 1.0)
        nc.vector.memset(f_scales_rest[:].bitcast(I32), 0)
        nc.scalar.activation(out=warm[:], in_=warm[:], func=ACT.Ln)
        make_identity(nc, ident[:])
        nc.gpsimd.memset(b_scales[:].bitcast(I32), 0)

        gain_view = log_gain.rearrange("c (g p t) -> p (c g) t", g=2, t=4)
        load_prior(0)
        load_scales(f_scales_first, fwd_scales[0:1])
        load_f(0)
        load_prior(1)
        nc.sync.dma_start(out=gain_first[:], in_=gain_view[:, 0:2, :])
        load_prior(2)
        load_prior(3)
        load_scales(f_scales_rest, fwd_scales[1:])
        load_f(1)
        nc.sync.dma_start(out=gain_rest[:], in_=gain_view[:, 2:, :])
        for c in (2, 3):
            load_prior(2 * c)
            load_prior(2 * c + 1)
            load_f(c)
        load_scales(b_scales, bwd_scales)
        for c in range(G):
            load_b(c)
        nc.sync.dma_start(out=self_raw[:, :, 0], in_=self_term.rearrange("c (j p) -> p (c j)", p=P))
        nc.sync.dma_start(out=factor_raw[:, :, 0], in_=input_factor.rearrange("c (j p) -> p (c j)", p=P))

        def prior_transpose(t):
            u, e = divmod(t, 2)
            bank = new_bank("tr", ("pt", t))
            words = prior_sb[u][:].bitcast(F32)
            for v in range(2):
                nc.tensor.transpose(bank[:, P * v : P * (v + 1)], words[:, e, v:256:2], ident[:])

        def prior_copy(t, eng):
            src = banks[("pt", t)][:, 0:256].rearrange("p (v r) -> p r v", v=2)
            dst = prior_t[t][:].bitcast(F32).rearrange("p (r v) -> p r v", v=2)
            if eng == "scalar":
                nc.scalar.copy(out=dst, in_=src)
            else:
                nc.vector.tensor_copy(out=dst, in_=src)

        def prior_quantize(t):
            nc.vector.quantize_mx(out=p_codes[t][:].bitcast(FP8X4), scales=p_scales[t][:], in_=prior_t[t][:])

        def mix_matmul(t, g):
            c = t // 4
            scales = f_scales_first[:, 0, :] if c == 0 else f_scales_rest[:, c - 1, :]
            bank = new_bank("mx", ("mix", t, g))
            nc.tensor.matmul_mx(
                out=bank[:],
                lhsT=p_codes[t][:].bitcast(FP8X4),
                lhsT_scale=p_scales[t][:],
                rhs=f_words[c][:, 1024 * g : 1024 * (g + 1)].bitcast(FP4X4),
                rhs_scale=scales[:, 512 * g : 512 * (g + 1)],
                start=True,
                stop=True,
            )

        def log_step(t, g):
            nc.scalar.activation(
                out=logs[(2 * t + g) % 16][:].rearrange("r (k p) -> r k p", k=4),
                in_=banks[("mix", t, g)][:].rearrange("r (p k) -> r k p", k=4),
                func=ACT.Ln,
            )

        def log_transpose(t, g):
            bank = new_bank("tr", ("lt", t, g))
            for k in range(4):
                cols = slice(P * k, P * (k + 1))
                nc.tensor.transpose(bank[:, cols], logs[(2 * t + g) % 16][:, cols], ident[:])

        def gain_step(t, g):
            u, e = divmod(t, 2)
            c = u // 2
            gain = gain_first[:, g, :] if c == 0 else gain_rest[:, 2 * (c - 1) + g, :]
            nc.vector.tensor_tensor(
                out=wlog[2 * u + g][:, 512 * e : 512 * (e + 1)].rearrange("p (r k) -> p r k", k=4),
                in0=banks[("lt", t, g)][:].rearrange("p (k r) -> p r k", k=4),
                in1=gain.unsqueeze(1).to_broadcast([P, P, 4]),
                op=ALU.mult,
            )

        def wlog_quantize(u, g):
            c, h = divmod(u, 2)
            cols = slice(256 * h, 256 * (h + 1))
            nc.vector.quantize_mx(
                out=w_codes[2 * c + g][:, cols].bitcast(FP8X4),
                scales=w_scales[2 * c + g][:, cols],
                in_=wlog[2 * u + g][:],
            )

        def cross_matmul(s):
            c, j = divmod(s, 4)
            bank = new_bank("mx", ("cross", s))
            for g in range(2):
                nc.tensor.matmul_mx(
                    out=bank[:],
                    lhsT=b_words[c][:, g, 256 * j : 256 * (j + 1)].bitcast(FP4X4),
                    lhsT_scale=b_scales[:, 2 * c + g, P * j : P * (j + 1)],
                    rhs=w_codes[2 * c + g][:].bitcast(FP8X4),
                    rhs_scale=w_scales[2 * c + g][:],
                    start=(g == 0),
                    stop=(g == 1),
                )

        def exp_step(s):
            nc.scalar.activation(
                out=expo[s][:], in_=banks[("cross", s)][:], func=ACT.Exp, bias=self_col[:, s : s + 1], scale=-1.0
            )

        def factor_step(s, eng):
            if eng == "scalar":
                nc.scalar.activation(
                    out=expo[s][:], in_=expo[s][:], func=ACT.Copy, scale=factor_col[:, s : s + 1]
                )
            else:
                nc.vector.tensor_scalar(
                    out=expo[s][:],
                    in0=expo[s][:],
                    scalar1=factor_col[:, s : s + 1],
                    scalar2=None,
                    op0=ALU.mult,
                )

        def exp_transpose(c, j0, j1, h):
            bank = new_bank("tr", ("et", c, j0, h))
            n = 0
            for e in range(2):
                for j in range(j0, j1):
                    r0 = 256 * h + P * e
                    nc.tensor.transpose(
                        bank[:, P * n : P * (n + 1)], expo[4 * c + j][:, r0 : r0 + P], ident[:]
                    )
                    n = n + 1

        def y_step(c, j0, j1, h):
            u = 2 * c + h
            cols = slice(P * j0, P * j1)
            nc.vector.tensor_tensor(
                out=y_sb[u][:, :, cols],
                in0=banks[("et", c, j0, h)][:, 0 : 2 * P * (j1 - j0)].rearrange("r (e i) -> r e i", e=2),
                in1=prior_sb[u][:, :, cols],
                op=ALU.mult,
            )

        def y_store(u, j0, j1):
            c, h = divmod(u, 2)
            cols = slice(P * j0, P * j1)
            rows = out_0[c, 256 * h : 256 * (h + 1), :].rearrange("(p e) i -> p e i", e=2)
            nc.sync.dma_start(out=rows[:, :, cols], in_=y_sb[u][:, :, cols])

        def y_round(u, j0, j1, eng):
            dst = y_bf[u][:].rearrange("r (v e p x) -> r v e p x", v=2, e=2, x=2)[:, :, :, 32 * j0 : 32 * j1, :]
            src = y_sb[u][:].rearrange("r e (p v x) -> r v e p x", v=2, x=2)[:, :, :, 32 * j0 : 32 * j1, :]
            if eng == "scalar":
                nc.scalar.copy(out=dst, in_=src)
            else:
                nc.vector.tensor_copy(out=dst, in_=src)

        def y_transpose(u):
            bank = new_bank("tr", ("yt", u))
            words = y_bf[u][:].bitcast(F32)
            for n in range(4):
                cols = slice(P * n, P * (n + 1))
                nc.tensor.transpose(bank[:, cols], words[:, cols], ident[:])

        def y_copy(u, eng):
            dst = y_t[u][:].bitcast(F32).rearrange("p (r e v) -> p r e v", e=2, v=2)
            src = banks[("yt", u)][:].rearrange("p (v e r) -> p r e v", v=2, e=2)
            if eng == "scalar":
                nc.scalar.copy(out=dst, in_=src)
            else:
                nc.vector.tensor_copy(out=dst, in_=src)

        def y_quantize(u):
            c, h = divmod(u, 2)
            nc.vector.quantize_mx(
                out=y_codes[c][:, 256 * h : 256 * (h + 1)].bitcast(FP8X4),
                scales=y_scales[:, 256 * u : 256 * (u + 1)],
                in_=y_t[u][:],
            )

        def codes_store(c, m0, m1):
            words = out_1[0].rearrange("p m t -> p (m t)").bitcast(I32)
            nc.sync.dma_start(out=words[:, R * c + m0 : R * c + m1], in_=y_codes[c][:, m0:m1].bitcast(I32))

        def scales_store():
            for q in range(4):
                eng = nc.sync if q % 2 == 0 else nc.scalar
                eng.dma_start(
                    out=out_2[0, 4 * q : 4 * q + 4, :].bitcast(I32), in_=y_scales[32 * q : 32 * q + 4, :].bitcast(I32)
                )

        def small_columns():
            nc.vector.tensor_copy(out=self_col[:], in_=self_raw[:, :, 0])
            nc.vector.tensor_copy(out=factor_col[:], in_=factor_raw[:, :, 0])

        def needs(step):
            fn, a = step[0], step[1:]
            if fn is prior_copy:
                return [(prior_transpose, a[0])]
            if fn is prior_quantize:
                return [(prior_copy, a[0])]
            if fn is mix_matmul:
                return [(prior_quantize, a[0])]
            if fn is log_step:
                return [(mix_matmul, a[0], a[1])] + ([(log_transpose, a[0] - 8, a[1])] if a[0] >= 8 else [])
            if fn is log_transpose:
                return [(log_step, a[0], a[1])]
            if fn is gain_step:
                return [(log_transpose, a[0], a[1])]
            if fn is wlog_quantize:
                return [(gain_step, 2 * a[0] + e, a[1]) for e in range(2)]
            if fn is cross_matmul:
                return [(wlog_quantize, 2 * (a[0] // 4) + h, g) for h in range(2) for g in range(2)]
            if fn is exp_step:
                return [(cross_matmul, a[0]), (small_columns,), (log_transpose, 8 + a[0] // 2, a[0] % 2)]
            if fn is factor_step:
                return [(exp_step, a[0])]
            if fn is exp_transpose:
                return [(factor_step, 4 * a[0] + j) for j in range(a[1], a[2])]
            if fn is y_step:
                return [(exp_transpose,) + a]
            if fn is y_store or fn is y_round:
                return [(y_step, a[0] // 2, j, j + 2, a[0] % 2) for j in range(a[1], a[2], 2)]
            if fn is y_transpose:
                return [(y_round, a[0], j0, j1) for (j0, j1) in round_parts(a[0])]
            if fn is y_copy:
                return [(y_transpose, a[0])]
            if fn is y_quantize:
                return [(y_copy, a[0])]
            if fn is codes_store:
                return [(y_quantize, 2 * a[0] + h) for h in range(a[1] // 256, a[2] // 256)]
            if fn is scales_store:
                return [(y_quantize, u) for u in range(UNITS)]
            return []

        def bank_reader(step):
            fn, a = step[0], step[1:]
            readers = {
                prior_transpose: prior_copy,
                mix_matmul: log_step,
                log_transpose: gain_step,
                cross_matmul: exp_step,
                exp_transpose: y_step,
                y_transpose: y_copy,
            }
            return (readers[fn],) + a

        def round_parts(u):
            return [(0, 2), (2, 4)] if u >= UNITS - 2 else [(0, 4)]

        either = (prior_copy, factor_step, y_round, y_copy)

        def weave(orders):
            done = set()
            tenants = {"mx": [], "tr": []}
            at = {name: 0 for name in orders}
            while any(at[name] < len(orders[name]) for name in orders):
                moved = False
                for name in orders:
                    while at[name] < len(orders[name]):
                        step = orders[name][at[name]]
                        wanted = needs(step)
                        if name == "tensor":
                            held = tenants["mx" if step[0] in (mix_matmul, cross_matmul) else "tr"]
                            if len(held) >= 4:
                                wanted = wanted + [bank_reader(held[-4])]
                        if not all(w in done for w in wanted):
                            break
                        if name == "tensor":
                            held.append(step)
                        args = step[1:] + ((name,) if step[0] in either else ())
                        step[0](*args)
                        done.add(step)
                        at[name] = at[name] + 1
                        moved = True
                assert moved, [orders[n][at[n]] for n in orders if at[n] < len(orders[n])]

        DOUBLE = (9, 12)
        EXTRA = (0, 1)
        FACTOR_S = (0, 1, 2, 4, 6, 8, 10, 12, 14)
        ROUND_S = (5,)
        LEAD = 2
        LR, LT, LC, LQ = 2, 3, 4, 5
        BEATS = 2 * G
        matmuls = [[(mix_matmul, t, 0), (mix_matmul, t, 1)] for t in range(TILES)]
        matmuls = matmuls + [[(cross_matmul, 2 * k), (cross_matmul, 2 * k + 1)] for k in range(BEATS)]
        pe = [(prior_transpose, 0), (prior_transpose, 1), (prior_transpose, 2)] + matmuls.pop(0) + matmuls.pop(0)
        act = [(prior_copy, 1), (log_step, 0, 0), (log_step, 0, 1), (log_step, 1, 0), (log_step, 1, 1)]
        dve = [(prior_copy, 0), (prior_quantize, 0), (prior_quantize, 1), (prior_copy, 2), (prior_quantize, 2)]
        sp = []
        turned = 3
        logged = 2
        mixed = 2
        waiting = []
        for t in range(TILES):
            pe.extend([(log_transpose, t, 0), (log_transpose, t, 1)])
            fresh = [n for n in range(turned, turned + (2 if t in EXTRA else 1)) if n < TILES]
            turned = turned + len(fresh)
            pe.extend([(prior_transpose, n) for n in fresh])
            act.extend([(prior_copy, n) for n in fresh])
            for rep in range(2 if t in DOUBLE else 1):
                if mixed < TILES + LEAD:
                    pe.extend(matmuls.pop(0))
                    mixed = mixed + 1
                if logged < TILES:
                    act.extend([(log_step, logged, 0), (log_step, logged, 1)])
                    logged = logged + 1
            dve.extend([(gain_step, t, 0), (gain_step, t, 1)])
            if t % 2 == 1:
                dve.append((wlog_quantize, t // 2, 0))
            elif t > 0:
                dve.append((wlog_quantize, t // 2 - 1, 1))
            dve.extend([(prior_quantize, n) for n in fresh])
            if t == 8:
                dve.append((small_columns,))
        late = [(wlog_quantize, UNITS - 1, 1)]

        while mixed < TILES + 3:
            pe.extend(matmuls.pop(0))
            mixed = mixed + 1
        for k in range(BEATS + 1):
            if k < BEATS:
                act.extend([(exp_step, 2 * k), (exp_step, 2 * k + 1)])
                act.extend([(factor_step, s) for s in (2 * k, 2 * k + 1) if s in FACTOR_S])
            if 0 <= k - LC < UNITS - 2:
                act.append((y_copy, k - LC))
            if k < BEATS:
                dve.extend([(factor_step, s) for s in (2 * k, 2 * k + 1) if s not in FACTOR_S])
            dve.extend(late)
            late = []
            if k >= 1:
                c, half = divmod(k - 1, 2)
                pe.extend([(exp_transpose, c, 2 * half, 2 * half + 2, h) for h in range(2)])
                dve.extend([(y_step, c, 2 * half, 2 * half + 2, h) for h in range(2)])
                if half == 1 and c < G - 1:
                    sp.extend([(y_store, 2 * c + h, 0, 4) for h in range(2)])
                if c == G - 1:
                    sp.extend([(y_store, 2 * c + h, 2 * half, 2 * half + 2) for h in range(2)])
            if 0 <= k - LT < UNITS - 2:
                pe.append((y_transpose, k - LT))
            if k >= 1 and matmuls:
                pe.extend(matmuls.pop(0))
            if 0 <= k - LQ < UNITS - 2:
                dve.append((y_quantize, k - LQ))
                if (k - LQ) % 2 == 1:
                    sp.append((codes_store, (k - LQ) // 2, 0, R))
            if 0 <= k - LR < UNITS - 2:
                (act if k - LR in ROUND_S else dve).append((y_round, k - LR, 0, 4))
            if k == BEATS - 1:
                act.extend([(y_round, 6, 0, 2), (y_round, 7, 0, 2)])
        k = BEATS + 1
        dve.extend([(y_round, 6, 2, 4), (y_round, 7, 2, 4)])
        pe.extend([(y_transpose, u) for u in range(k - LT, UNITS - 2)] + [(y_transpose, 6), (y_transpose, 7)])
        act.extend([(y_copy, u) for u in range(k - LC, UNITS - 1)])
        dve.extend([(y_quantize, u) for u in range(k - LQ, UNITS - 2)])
        dve.extend([(y_copy, 7), (y_quantize, 6), (y_quantize, 7)])
        sp.extend([(codes_store, c, 0, R) for c in range((k - LQ) // 2, G)] + [(scales_store,)])
        weave({"tensor": pe, "scalar": act, "vector": dve, "sync": sp})
